import numpy as np
import ml_dtypes


def mxq(x, axis, fmt="e4m3"):
    dtype, down = {"e4m3": (ml_dtypes.float8_e4m3fn, 7), "e5m2": (ml_dtypes.float8_e5m2, 14)}[fmt]
    v = np.moveaxis(np.asarray(x, np.float32).astype(ml_dtypes.bfloat16).astype(np.float64), axis, -1)
    blocks = v.reshape(v.shape[:-1] + (-1, 32))
    amax = np.abs(blocks).max(-1, keepdims=True)
    byte = np.maximum(np.where(amax > 0, np.frexp(amax)[1] - 1 + 127, 0) - down, 1)
    scale = np.exp2(byte - 127.0)
    codes = (blocks / scale).astype(np.float32).astype(dtype).astype(np.float64)
    return np.moveaxis((codes * scale).reshape(v.shape), -1, axis)


WIDE = False


def mx_kscale(k):
    if not WIDE:
        return np.ones(k)
    levels = np.array([10, -10, 5, -5, 0])
    if k % 512:
        return np.exp2(np.random.permutation(np.resize(levels, k // 32))).repeat(32)
    a = np.empty((k // 512, 16))
    for p in range(k // 512):
        a[p, :8] = np.random.permutation(np.resize(levels, 8))
        for g in range(8):
            far = levels[np.abs(levels - a[p, g]) >= 10]
            a[p, g + 8] = far[np.random.randint(len(far))]
    return np.exp2(a.ravel()).repeat(32)


def f64(x):
    return np.asarray(x).astype(np.float64)


def striped8(idx):
    return np.asarray(idx).reshape(8, -1, 16).transpose(0, 2, 1).reshape(128, -1).astype(np.uint16)


def unstriped8(offs):
    return offs.reshape(8, 16, -1).transpose(0, 2, 1).reshape(8, -1).astype(np.int64)


def pick8(x, idx, run):
    r = np.arange(len(x))
    return x[r[:, None], idx[r % (8 * run) // run]]


E2M1 = np.array([0.0, 0.5, 1.0, 1.5, 2.0, 3.0, 4.0, 6.0, -0.0, -0.5, -1.0, -1.5, -2.0, -3.0, -4.0, -6.0])


def pack_weight(w, fmt):
    k, n = w.shape
    w = f64(np.asarray(w, np.float32).astype(ml_dtypes.bfloat16)).reshape(k // 32, 32, n)
    amax = np.abs(w).max(1)
    if fmt == "e4m3":
        byte = np.frexp(amax)[1] - 1 + 127 - 7
    else:
        mant, ex = np.frexp(amax / 6.0)
        byte = np.where(mant > 0.5, ex, ex - 1) + 127
    byte = np.clip(np.where(amax > 0, byte, 1), 1, 254)
    scaled = (w * np.exp2(127.0 - byte)[:, None, :]).reshape(k, n).astype(np.float32)
    by_word = np.ascontiguousarray(scaled.reshape(k // 512, 128, 4, n).transpose(0, 1, 3, 2))
    if fmt == "e4m3":
        words = by_word.astype(ml_dtypes.float8_e4m3fn).view(np.uint8)
    else:
        c = by_word.astype(ml_dtypes.float4_e2m1fn).view(np.uint8) & 0xF
        words = (c[..., 0::2] | (c[..., 1::2] << 4)).reshape(k // 512, 128, 2 * n)
    return np.ascontiguousarray(words), np.ascontiguousarray(byte.astype(np.uint8).reshape(k // 512, 16, n))


def unpack_weight(words, scales, fmt):
    g, _, n = scales.shape
    words = np.ascontiguousarray(words).reshape(g, 128, n, -1)
    if fmt == "e4m3":
        vals = words.view(ml_dtypes.float8_e4m3fn).astype(np.float64)
    else:
        nib = np.empty((g, 128, n, 4), np.uint8)
        nib[..., 0::2] = words & 0xF
        nib[..., 1::2] = words >> 4
        vals = E2M1[nib]
    vals = vals * np.repeat(np.exp2(scales.astype(np.float64) - 127.0), 8, axis=1)[..., None]
    return vals.transpose(0, 1, 3, 2).reshape(g * 512, n)


D, T, U, X, I, Q = 512, 1024, 1024, 1024, 512, 128


def setup_inputs():
    n = np.random.standard_normal
    idx = np.stack([np.random.permutation(T)[:I] for _ in range(8)])
    idx2 = np.stack([np.random.permutation(X)[:I] for _ in range(8)])
    idx3 = np.stack([np.random.permutation(U)[:I] for _ in range(8)])
    idx4 = np.stack([np.random.permutation(X)[:I] for _ in range(8)])
    idx5 = np.stack([np.random.permutation(X)[:I] for _ in range(8)])
    fd = mx_kscale(D)
    keysp = pack_weight(n((D, T)) / fd[:, None], "e2m1")
    notesp = pack_weight(n((D, U)) / fd[:, None], "e4m3")
    usersp = pack_weight(n((D, X)) / fd[:, None], "e2m1")
    return {
        "query": (n((D, Q)) * 1.0 / np.sqrt(D) * fd[:, None]).astype(np.float32),
        "keys_words": keysp[0],
        "keys_scales": keysp[1],
        "notes_words": notesp[0],
        "notes_scales": notesp[1],
        "users_words": usersp[0],
        "users_scales": usersp[1],
        "lam": (np.random.uniform(0.5, 1.5, (Q, 1))).astype(np.float32),
        "offs": striped8(idx),
        "offs2": striped8(idx2),
        "offs3": striped8(idx3),
        "offs4": striped8(idx4),
        "offs5": striped8(idx5),
    }


def reference(query, keys_words, keys_scales, notes_words, notes_scales, users_words, users_scales, lam, offs, offs2, offs3, offs4, offs5):
    idx = unstriped8(offs)
    idx2 = unstriped8(offs2)
    idx3 = unstriped8(offs3)
    idx4 = unstriped8(offs4)
    idx5 = unstriped8(offs5)
    keysu = unpack_weight(keys_words, keys_scales, "e2m1")
    notesu = unpack_weight(notes_words, notes_scales, "e4m3")
    usersu = unpack_weight(users_words, users_scales, "e2m1")
    queryq = mxq(f64(query), 0, "e4m3")
    a = queryq.T @ keysu
    b = queryq.T @ notesu
    c0 = queryq.T @ usersu
    f1 = np.zeros((Q, X))
    f1[np.arange(Q)[:, None], idx2[np.arange(Q) % 128 // 16]] = pick8(a, idx, 16)
    f2 = np.zeros((Q, X))
    f2[np.arange(Q)[:, None], idx4[np.arange(Q) % 128 // 16]] = pick8(b, idx3, 16)
    r = np.maximum(f1, f2 * f64(lam))
    cc = c0 + r
    y = pick8(cc, idx5, 16)
    return y

@@ -1,0 +1,129 @@
+from contextlib import ExitStack
+
+import concourse.mybir as mybir
+
+D, T, I, Q = 512, 1024, 512, 128
+FLOPS = 2 * D * Q * 3 * T
+
+F32 = mybir.dt.float32
+BF16 = mybir.dt.bfloat16
+I32 = mybir.dt.int32
+U32 = mybir.dt.uint32
+U16 = mybir.dt.uint16
+U8 = mybir.dt.uint8
+FP8X4 = mybir.dt.float8_e4m3fn_x4
+FP4X4 = mybir.dt.float4_e2m1fn_x4
+COPY = mybir.ActivationFunctionType.Copy
+ALU = mybir.AluOpType
+
+P = 128
+PACK = 4
+LIST_COLS = I // 16
+HALF = I // 2
+
+
+def tile_attend_twocourts_three_kernel(tc, query, keys_words, keys_scales, notes_words, notes_scales,
+                                        users_words, users_scales, lam, offs, offs2, offs3, offs4, offs5, out):
+    nc = tc.nc
+    with ExitStack() as ctx:
+        held = ctx.enter_context(tc.tile_pool(name="held", bufs=1))
+        psum = ctx.enter_context(tc.psum_pool(name="psum", bufs=1))
+
+        def plane(name):
+            tile = held.tile([P, T], U8, name=name, align_bytes=64)
+            nc.vector.memset(tile[:].bitcast(I32), 0)
+            return tile
+
+        def load_plane(tile, scales):
+            for quad in range(4):
+                nc.sync.dma_start(tile[32 * quad : 32 * quad + 4, :].bitcast(I32),
+                                  scales[0, 4 * quad : 4 * quad + 4, :].bitcast(I32))
+
+        def load_list(name, src):
+            tile = held.tile([P, LIST_COLS], U16, name=name)
+            nc.sync.dma_start(tile[:], src)
+            return tile
+
+        keys_plane = plane("keys_plane")
+        notes_plane = plane("notes_plane")
+        users_plane = plane("users_plane")
+        f1 = held.tile([P, T], F32, name="f1")
+        f2 = held.tile([P, T], F32, name="f2")
+        nc.vector.memset(f1[:].bitcast(I32), 0)
+        nc.vector.memset(f2[:].bitcast(I32), 0)
+
+        q_raw = held.tile([P, PACK, Q], F32, name="q_raw")
+        nc.sync.dma_start(q_raw[:], query.rearrange("(p j) w -> p j w", j=PACK))
+        keys_w = held.tile([P, 2 * T], U8, name="keys_w", align_bytes=64)
+        nc.sync.dma_start(keys_w[:].bitcast(I32), keys_words[0].bitcast(I32))
+        load_plane(keys_plane, keys_scales)
+        list1 = load_list("list1", offs)
+        notes_w = held.tile([P, T], U32, name="notes_w", align_bytes=64)
+        nc.sync.dma_start(notes_w[:].bitcast(I32), notes_words[0].rearrange("p n t -> p (n t)").bitcast(I32))
+        list2 = load_list("list2", offs2)
+        load_plane(notes_plane, notes_scales)
+        list3 = load_list("list3", offs3)
+        list4 = load_list("list4", offs4)
+        users_w = held.tile([P, 2 * T], U8, name="users_w", align_bytes=64)
+        nc.sync.dma_start(users_w[:].bitcast(I32), users_words[0].bitcast(I32))
+        load_plane(users_plane, users_scales)
+        lam_sb = held.tile([P, 1], F32, name="lam_sb")
+        nc.sync.dma_start(lam_sb[:], lam)
+        list5 = load_list("list5", offs5)
+
+        q_bf = held.tile([P, Q, PACK], BF16, name="q_bf", align_bytes=64)
+        nc.vector.tensor_copy(q_bf[:].rearrange("p (c i) t -> p c t i", i=4),
+                              q_raw[:].rearrange("p t (c i) -> p c t i", i=4))
+        q_codes = held.tile([P, Q], U32, name="q_codes", align_bytes=64)
+        q_plane = held.tile([P, Q], U8, name="q_plane", align_bytes=64)
+        nc.vector.quantize_mx(out=q_codes[:].bitcast(FP8X4), scales=q_plane[:],
+                              in_=q_bf[:].rearrange("p w j -> p (w j)"))
+
+        def score(name, rhs, rhs_scale, width):
+            bank = psum.tile([P, width], F32, name=name)
+            nc.tensor.matmul_mx(out=bank[:], lhsT=q_codes[:].bitcast(FP8X4), lhsT_scale=q_plane[:],
+                                rhs=rhs, rhs_scale=rhs_scale, start=True, stop=True)
+            return bank
+
+        a = held.tile([P, T], F32, name="a")
+        piece = T // 4
+        for n in range(4):
+            cols = slice(n * piece, (n + 1) * piece)
+            bank = score("a_bank%d" % n, keys_w[:, 2 * n * piece : 2 * (n + 1) * piece].bitcast(FP4X4),
+                         keys_plane[:, cols], piece)
+            if n % 2 == 0:
+                nc.scalar.copy(a[:, cols], bank[:])
+            else:
+                nc.vector.tensor_copy(a[:, cols], bank[:])
+
+        picked_a = held.tile([P, I], F32, name="picked_a")
+        nc.vector.tensor_copy(picked_a[:, :HALF], a[:].indirect(list1[:, : LIST_COLS // 2]))
+        nc.scalar.activation(picked_a[:, HALF:], a[:].indirect(list1[:, LIST_COLS // 2 :]), COPY)
+        nc.vector.tensor_copy(f1[:].indirect(list2[:]), picked_a[:])
+
+        b = held.tile([P, T], F32, name="b")
+        for n in range(2):
+            cols = slice(n * 512, (n + 1) * 512)
+            bank = score("b_bank%d" % n, notes_w[:, cols].bitcast(FP8X4), notes_plane[:, cols], 512)
+            nc.scalar.copy(b[:, cols], bank[:])
+        picked_b = held.tile([P, I], F32, name="picked_b")
+        nc.scalar.activation(picked_b[:], b[:].indirect(list3[:]), COPY)
+        nc.vector.tensor_copy(f2[:].indirect(list4[:]), picked_b[:])
+
+        r = held.tile([P, T], F32, name="r")
+        for n in range(2):
+            cols = slice(n * 512, (n + 1) * 512)
+            nc.vector.scalar_tensor_tensor(r[:, cols], f2[:, cols], lam_sb[:], f1[:, cols], ALU.mult, ALU.max)
+        cc = held.tile([P, T], F32, name="cc")
+        for n in range(2):
+            cols = slice(n * 512, (n + 1) * 512)
+            bank = score("c_bank%d" % n, users_w[:, 1024 * n : 1024 * (n + 1)].bitcast(FP4X4),
+                         users_plane[:, cols], 512)
+            nc.vector.tensor_tensor(cc[:, cols], r[:, cols], bank[:], ALU.add)
+
+        y0 = held.tile([P, HALF], F32, name="y0")
+        y1 = held.tile([P, HALF], F32, name="y1")
+        nc.vector.tensor_copy(y0[:], cc[:].indirect(list5[:, : LIST_COLS // 2]))
+        nc.scalar.activation(y1[:], cc[:].indirect(list5[:, LIST_COLS // 2 :]), COPY)
+        nc.sync.dma_start(out[:, :HALF], y0[:])
+        nc.scalar.dma_start(out[:, HALF:], y1[:])

@@ -20,6 +20,8 @@ P = 128
 PACK = 4
 LIST_COLS = I // 16
 HALF = I // 2
+CAST_SPLIT = 80
+SHARE = 224
 
 
 def tile_attend_twocourts_three_kernel(tc, query, keys_words, keys_scales, notes_words, notes_scales,
@@ -48,20 +50,18 @@ def tile_attend_twocourts_three_kernel(tc, query, keys_words, keys_scales, notes
         notes_plane = plane("notes_plane")
         users_plane = plane("users_plane")
         f1 = held.tile([P, T], F32, name="f1")
-        f2 = held.tile([P, T], F32, name="f2")
         nc.vector.memset(f1[:].bitcast(I32), 0)
-        nc.vector.memset(f2[:].bitcast(I32), 0)
 
         q_raw = held.tile([P, PACK, Q], F32, name="q_raw")
         nc.sync.dma_start(q_raw[:], query.rearrange("(p j) w -> p j w", j=PACK))
         keys_w = held.tile([P, 2 * T], U8, name="keys_w", align_bytes=64)
         nc.sync.dma_start(keys_w[:].bitcast(I32), keys_words[0].bitcast(I32))
         load_plane(keys_plane, keys_scales)
-        list1 = load_list("list1", offs)
         notes_w = held.tile([P, T], U32, name="notes_w", align_bytes=64)
         nc.sync.dma_start(notes_w[:].bitcast(I32), notes_words[0].rearrange("p n t -> p (n t)").bitcast(I32))
-        list2 = load_list("list2", offs2)
+        list1 = load_list("list1", offs)
         load_plane(notes_plane, notes_scales)
+        list2 = load_list("list2", offs2)
         list3 = load_list("list3", offs3)
         list4 = load_list("list4", offs4)
         users_w = held.tile([P, 2 * T], U8, name="users_w", align_bytes=64)
@@ -71,26 +71,31 @@ def tile_attend_twocourts_three_kernel(tc, query, keys_words, keys_scales, notes
         nc.sync.dma_start(lam_sb[:], lam)
         list5 = load_list("list5", offs5)
 
-        q_bf = held.tile([P, Q, PACK], BF16, name="q_bf", align_bytes=64)
-        nc.vector.tensor_copy(q_bf[:].rearrange("p (c i) t -> p c t i", i=4),
-                              q_raw[:].rearrange("p t (c i) -> p c t i", i=4))
+        q_bf = held.tile([P, Q, PACK], BF16, name="q_bf", tag="reused", align_bytes=64)
+        nc.vector.tensor_copy(q_bf[:, :CAST_SPLIT, :].rearrange("p (c i) t -> p c t i", i=4),
+                              q_raw[:, :, :CAST_SPLIT].rearrange("p t (c i) -> p c t i", i=4))
+        nc.scalar.copy(q_bf[:, CAST_SPLIT:, :].rearrange("p (c i) t -> p c t i", i=4),
+                       q_raw[:, :, CAST_SPLIT:].rearrange("p t (c i) -> p c t i", i=4))
         q_codes = held.tile([P, Q], U32, name="q_codes", align_bytes=64)
         q_plane = held.tile([P, Q], U8, name="q_plane", align_bytes=64)
         nc.vector.quantize_mx(out=q_codes[:].bitcast(FP8X4), scales=q_plane[:],
                               in_=q_bf[:].rearrange("p w j -> p (w j)"))
 
-        def score(name, rhs, rhs_scale, width):
-            bank = psum.tile([P, width], F32, name=name)
+        f2 = held.tile([P, T], F32, name="f2", tag="reused", align_bytes=64)
+        nc.vector.memset(f2[:].bitcast(I32), 0)
+
+        def score(name, tag, rhs, rhs_scale, width):
+            bank = psum.tile([P, width], F32, name=name, tag=tag)
             nc.tensor.matmul_mx(out=bank[:], lhsT=q_codes[:].bitcast(FP8X4), lhsT_scale=q_plane[:],
                                 rhs=rhs, rhs_scale=rhs_scale, start=True, stop=True)
             return bank
 
         a = held.tile([P, T], F32, name="a")
-        piece = T // 4
-        for n in range(4):
-            cols = slice(n * piece, (n + 1) * piece)
-            bank = score("a_bank%d" % n, keys_w[:, 2 * n * piece : 2 * (n + 1) * piece].bitcast(FP4X4),
-                         keys_plane[:, cols], piece)
+        edges = (0, 256, 512, 768, 896, 1024)
+        for n in range(5):
+            cols = slice(edges[n], edges[n + 1])
+            bank = score("a_bank%d" % n, "bank%d" % n, keys_w[:, 2 * cols.start : 2 * cols.stop].bitcast(FP4X4),
+                         keys_plane[:, cols], cols.stop - cols.start)
             if n % 2 == 0:
                 nc.scalar.copy(a[:, cols], bank[:])
             else:
@@ -101,25 +106,26 @@ def tile_attend_twocourts_three_kernel(tc, query, keys_words, keys_scales, notes
         nc.scalar.activation(picked_a[:, HALF:], a[:].indirect(list1[:, LIST_COLS // 2 :]), COPY)
         nc.vector.tensor_copy(f1[:].indirect(list2[:]), picked_a[:])
 
-        b = held.tile([P, T], F32, name="b")
+        b = held.tile([P, T], F32, name="b", tag="b")
         for n in range(2):
             cols = slice(n * 512, (n + 1) * 512)
-            bank = score("b_bank%d" % n, notes_w[:, cols].bitcast(FP8X4), notes_plane[:, cols], 512)
+            bank = score("b_bank%d" % n, "bank%d" % (5 + n), notes_w[:, cols].bitcast(FP8X4), notes_plane[:, cols], 512)
             nc.scalar.copy(b[:, cols], bank[:])
         picked_b = held.tile([P, I], F32, name="picked_b")
         nc.scalar.activation(picked_b[:], b[:].indirect(list3[:]), COPY)
         nc.vector.tensor_copy(f2[:].indirect(list4[:]), picked_b[:])
 
+        c_banks = [score("c_bank%d" % n, "bank%d" % (7 * n), users_w[:, 1024 * n : 1024 * (n + 1)].bitcast(FP4X4),
+                         users_plane[:, n * 512 : (n + 1) * 512], 512) for n in range(2)]
+        c_head = held.tile([P, SHARE], F32, name="c_head", tag="b")
+        nc.scalar.copy(c_head[:], c_banks[0][:, :SHARE])
         r = held.tile([P, T], F32, name="r")
-        for n in range(2):
-            cols = slice(n * 512, (n + 1) * 512)
+        for cols in (slice(SHARE, 512), slice(512, T), slice(0, SHARE)):
             nc.vector.scalar_tensor_tensor(r[:, cols], f2[:, cols], lam_sb[:], f1[:, cols], ALU.mult, ALU.max)
         cc = held.tile([P, T], F32, name="cc")
-        for n in range(2):
-            cols = slice(n * 512, (n + 1) * 512)
-            bank = score("c_bank%d" % n, users_w[:, 1024 * n : 1024 * (n + 1)].bitcast(FP4X4),
-                         users_plane[:, cols], 512)
-            nc.vector.tensor_tensor(cc[:, cols], r[:, cols], bank[:], ALU.add)
+        nc.gpsimd.tensor_tensor(cc[:, :SHARE], r[:, :SHARE], c_head[:], ALU.add)
+        nc.vector.tensor_tensor(cc[:, SHARE:512], r[:, SHARE:512], c_banks[0][:, SHARE:], ALU.add)
+        nc.vector.tensor_tensor(cc[:, 512:], r[:, 512:], c_banks[1][:], ALU.add)
 
         y0 = held.tile([P, HALF], F32, name="y0")
         y1 = held.tile([P, HALF], F32, name="y1")

@@ -54,9 +54,10 @@ def tile_attend_twocourts_three_kernel(tc, query, keys_words, keys_scales, notes
 
         q_raw = held.tile([P, PACK, Q], F32, name="q_raw")
         nc.sync.dma_start(q_raw[:], query.rearrange("(p j) w -> p j w", j=PACK))
-        keys_w = held.tile([P, 2 * T], U8, name="keys_w", align_bytes=64)
-        nc.sync.dma_start(keys_w[:].bitcast(I32), keys_words[0].bitcast(I32))
+        keys_w = [held.tile([P, T], U8, name="keys_w%d" % n, align_bytes=64) for n in range(2)]
+        nc.sync.dma_start(keys_w[0][:].bitcast(I32), keys_words[0][:, :T].bitcast(I32))
         load_plane(keys_plane, keys_scales)
+        nc.sync.dma_start(keys_w[1][:].bitcast(I32), keys_words[0][:, T:].bitcast(I32))
         notes_w = held.tile([P, T], U32, name="notes_w", align_bytes=64)
         nc.sync.dma_start(notes_w[:].bitcast(I32), notes_words[0].rearrange("p n t -> p (n t)").bitcast(I32))
         list1 = load_list("list1", offs)
@@ -94,7 +95,9 @@ def tile_attend_twocourts_three_kernel(tc, query, keys_words, keys_scales, notes
         edges = (0, 256, 512, 768, 896, 1024)
         for n in range(5):
             cols = slice(edges[n], edges[n + 1])
-            bank = score("a_bank%d" % n, "bank%d" % n, keys_w[:, 2 * cols.start : 2 * cols.stop].bitcast(FP4X4),
+            half, first = divmod(cols.start, 512)
+            words = keys_w[half][:, 2 * first : 2 * (first + cols.stop - cols.start)]
+            bank = score("a_bank%d" % n, "bank%d" % n, words.bitcast(FP4X4),
                          keys_plane[:, cols], cols.stop - cols.start)
             if n % 2 == 0:
                 nc.scalar.copy(a[:, cols], bank[:])

from contextlib import ExitStack

import concourse.mybir as mybir

D, T, I, Q = 512, 1024, 512, 128
FLOPS = 2 * D * Q * 3 * T

F32 = mybir.dt.float32
BF16 = mybir.dt.bfloat16
I32 = mybir.dt.int32
U32 = mybir.dt.uint32
U16 = mybir.dt.uint16
U8 = mybir.dt.uint8
FP8X4 = mybir.dt.float8_e4m3fn_x4
FP4X4 = mybir.dt.float4_e2m1fn_x4
COPY = mybir.ActivationFunctionType.Copy
ALU = mybir.AluOpType

P = 128
PACK = 4
LIST_COLS = I // 16
HALF = I // 2
CAST_SPLIT = 80
SHARE = 224


def tile_attend_twocourts_three_kernel(tc, query, keys_words, keys_scales, notes_words, notes_scales,
                                        users_words, users_scales, lam, offs, offs2, offs3, offs4, offs5, out):
    nc = tc.nc
    with ExitStack() as ctx:
        held = ctx.enter_context(tc.tile_pool(name="held", bufs=1))
        psum = ctx.enter_context(tc.psum_pool(name="psum", bufs=1))

        def plane(name):
            tile = held.tile([P, T], U8, name=name, align_bytes=64)
            nc.vector.memset(tile[:].bitcast(I32), 0)
            return tile

        def load_plane(tile, scales):
            for quad in range(4):
                nc.sync.dma_start(tile[32 * quad : 32 * quad + 4, :].bitcast(I32),
                                  scales[0, 4 * quad : 4 * quad + 4, :].bitcast(I32))

        def load_list(name, src):
            tile = held.tile([P, LIST_COLS], U16, name=name)
            nc.sync.dma_start(tile[:], src)
            return tile

        keys_plane = plane("keys_plane")
        notes_plane = plane("notes_plane")
        users_plane = plane("users_plane")
        f1 = held.tile([P, T], F32, name="f1")
        nc.vector.memset(f1[:].bitcast(I32), 0)

        q_raw = held.tile([P, PACK, Q], F32, name="q_raw")
        nc.sync.dma_start(q_raw[:], query.rearrange("(p j) w -> p j w", j=PACK))
        keys_w = [held.tile([P, T], U8, name="keys_w%d" % n, align_bytes=64) for n in range(2)]
        nc.sync.dma_start(keys_w[0][:].bitcast(I32), keys_words[0][:, :T].bitcast(I32))
        load_plane(keys_plane, keys_scales)
        nc.sync.dma_start(keys_w[1][:].bitcast(I32), keys_words[0][:, T:].bitcast(I32))
        notes_w = held.tile([P, T], U32, name="notes_w", align_bytes=64)
        nc.sync.dma_start(notes_w[:].bitcast(I32), notes_words[0].rearrange("p n t -> p (n t)").bitcast(I32))
        list1 = load_list("list1", offs)
        load_plane(notes_plane, notes_scales)
        list2 = load_list("list2", offs2)
        list3 = load_list("list3", offs3)
        list4 = load_list("list4", offs4)
        users_w = held.tile([P, 2 * T], U8, name="users_w", align_bytes=64)
        nc.sync.dma_start(users_w[:].bitcast(I32), users_words[0].bitcast(I32))
        load_plane(users_plane, users_scales)
        lam_sb = held.tile([P, 1], F32, name="lam_sb")
        nc.sync.dma_start(lam_sb[:], lam)
        list5 = load_list("list5", offs5)

        q_bf = held.tile([P, Q, PACK], BF16, name="q_bf", tag="reused", align_bytes=64)
        nc.vector.tensor_copy(q_bf[:, :CAST_SPLIT, :].rearrange("p (c i) t -> p c t i", i=4),
                              q_raw[:, :, :CAST_SPLIT].rearrange("p t (c i) -> p c t i", i=4))
        nc.scalar.copy(q_bf[:, CAST_SPLIT:, :].rearrange("p (c i) t -> p c t i", i=4),
                       q_raw[:, :, CAST_SPLIT:].rearrange("p t (c i) -> p c t i", i=4))
        q_codes = held.tile([P, Q], U32, name="q_codes", align_bytes=64)
        q_plane = held.tile([P, Q], U8, name="q_plane", align_bytes=64)
        nc.vector.quantize_mx(out=q_codes[:].bitcast(FP8X4), scales=q_plane[:],
                              in_=q_bf[:].rearrange("p w j -> p (w j)"))

        f2 = held.tile([P, T], F32, name="f2", tag="reused", align_bytes=64)
        nc.vector.memset(f2[:].bitcast(I32), 0)

        def score(name, tag, rhs, rhs_scale, width):
            bank = psum.tile([P, width], F32, name=name, tag=tag)
            nc.tensor.matmul_mx(out=bank[:], lhsT=q_codes[:].bitcast(FP8X4), lhsT_scale=q_plane[:],
                                rhs=rhs, rhs_scale=rhs_scale, start=True, stop=True)
            return bank

        a = held.tile([P, T], F32, name="a")
        edges = (0, 256, 512, 768, 896, 1024)
        for n in range(5):
            cols = slice(edges[n], edges[n + 1])
            half, first = divmod(cols.start, 512)
            words = keys_w[half][:, 2 * first : 2 * (first + cols.stop - cols.start)]
            bank = score("a_bank%d" % n, "bank%d" % n, words.bitcast(FP4X4),
                         keys_plane[:, cols], cols.stop - cols.start)
            if n % 2 == 0:
                nc.scalar.copy(a[:, cols], bank[:])
            else:
                nc.vector.tensor_copy(a[:, cols], bank[:])

        picked_a = held.tile([P, I], F32, name="picked_a")
        nc.vector.tensor_copy(picked_a[:, :HALF], a[:].indirect(list1[:, : LIST_COLS // 2]))
        nc.scalar.activation(picked_a[:, HALF:], a[:].indirect(list1[:, LIST_COLS // 2 :]), COPY)
        nc.vector.tensor_copy(f1[:].indirect(list2[:]), picked_a[:])

        b = held.tile([P, T], F32, name="b", tag="b")
        for n in range(2):
            cols = slice(n * 512, (n + 1) * 512)
            bank = score("b_bank%d" % n, "bank%d" % (5 + n), notes_w[:, cols].bitcast(FP8X4), notes_plane[:, cols], 512)
            nc.scalar.copy(b[:, cols], bank[:])
        picked_b = held.tile([P, I], F32, name="picked_b")
        nc.scalar.activation(picked_b[:], b[:].indirect(list3[:]), COPY)
        nc.vector.tensor_copy(f2[:].indirect(list4[:]), picked_b[:])

        c_banks = [score("c_bank%d" % n, "bank%d" % (7 * n), users_w[:, 1024 * n : 1024 * (n + 1)].bitcast(FP4X4),
                         users_plane[:, n * 512 : (n + 1) * 512], 512) for n in range(2)]
        c_head = held.tile([P, SHARE], F32, name="c_head", tag="b")
        nc.scalar.copy(c_head[:], c_banks[0][:, :SHARE])
        r = held.tile([P, T], F32, name="r")
        for cols in (slice(SHARE, 512), slice(512, T), slice(0, SHARE)):
            nc.vector.scalar_tensor_tensor(r[:, cols], f2[:, cols], lam_sb[:], f1[:, cols], ALU.mult, ALU.max)
        cc = held.tile([P, T], F32, name="cc")
        nc.gpsimd.tensor_tensor(cc[:, :SHARE], r[:, :SHARE], c_head[:], ALU.add)
        nc.vector.tensor_tensor(cc[:, SHARE:512], r[:, SHARE:512], c_banks[0][:, SHARE:], ALU.add)
        nc.vector.tensor_tensor(cc[:, 512:], r[:, 512:], c_banks[1][:], ALU.add)

        y0 = held.tile([P, HALF], F32, name="y0")
        y1 = held.tile([P, HALF], F32, name="y1")
        nc.vector.tensor_copy(y0[:], cc[:].indirect(list5[:, : LIST_COLS // 2]))
        nc.scalar.activation(y1[:], cc[:].indirect(list5[:, LIST_COLS // 2 :]), COPY)
        nc.sync.dma_start(out[:, :HALF], y0[:])
        nc.scalar.dma_start(out[:, HALF:], y1[:])
